import numpy as np
import ml_dtypes


def mxq(x, axis, fmt="e4m3"):
    dtype, down = {"e4m3": (ml_dtypes.float8_e4m3fn, 7), "e5m2": (ml_dtypes.float8_e5m2, 14)}[fmt]
    v = np.moveaxis(np.asarray(x, np.float32).astype(ml_dtypes.bfloat16).astype(np.float64), axis, -1)
    blocks = v.reshape(v.shape[:-1] + (-1, 32))
    amax = np.abs(blocks).max(-1, keepdims=True)
    byte = np.maximum(np.where(amax > 0, np.frexp(amax)[1] - 1 + 127, 0) - down, 1)
    scale = np.exp2(byte - 127.0)
    codes = (blocks / scale).astype(np.float32).astype(dtype).astype(np.float64)
    return np.moveaxis((codes * scale).reshape(v.shape), -1, axis)


WIDE = False


def mx_kscale(k):
    if not WIDE:
        return np.ones(k)
    levels = np.array([10, -10, 5, -5, 0])
    if k % 512:
        return np.exp2(np.random.permutation(np.resize(levels, k // 32))).repeat(32)
    a = np.empty((k // 512, 16))
    for p in range(k // 512):
        a[p, :8] = np.random.permutation(np.resize(levels, 8))
        for g in range(8):
            far = levels[np.abs(levels - a[p, g]) >= 10]
            a[p, g + 8] = far[np.random.randint(len(far))]
    return np.exp2(a.ravel()).repeat(32)


def f64(x):
    return np.asarray(x).astype(np.float64)


def striped(idx):
    return np.tile(idx.reshape(-1, 16).T, (8, 1)).astype(np.uint16)


def unstriped(offs):
    return offs[:16].T.reshape(-1).astype(np.int64)


E2M1 = np.array([0.0, 0.5, 1.0, 1.5, 2.0, 3.0, 4.0, 6.0, -0.0, -0.5, -1.0, -1.5, -2.0, -3.0, -4.0, -6.0])


def pack_weight(w, fmt):
    k, n = w.shape
    w = f64(np.asarray(w, np.float32).astype(ml_dtypes.bfloat16)).reshape(k // 32, 32, n)
    amax = np.abs(w).max(1)
    if fmt == "e4m3":
        byte = np.frexp(amax)[1] - 1 + 127 - 7
    else:
        mant, ex = np.frexp(amax / 6.0)
        byte = np.where(mant > 0.5, ex, ex - 1) + 127
    byte = np.clip(np.where(amax > 0, byte, 1), 1, 254)
    scaled = (w * np.exp2(127.0 - byte)[:, None, :]).reshape(k, n).astype(np.float32)
    by_word = np.ascontiguousarray(scaled.reshape(k // 512, 128, 4, n).transpose(0, 1, 3, 2))
    if fmt == "e4m3":
        words = by_word.astype(ml_dtypes.float8_e4m3fn).view(np.uint8)
    else:
        c = by_word.astype(ml_dtypes.float4_e2m1fn).view(np.uint8) & 0xF
        words = (c[..., 0::2] | (c[..., 1::2] << 4)).reshape(k // 512, 128, 2 * n)
    return np.ascontiguousarray(words), np.ascontiguousarray(byte.astype(np.uint8).reshape(k // 512, 16, n))


def unpack_weight(words, scales, fmt):
    g, _, n = scales.shape
    words = np.ascontiguousarray(words).reshape(g, 128, n, -1)
    if fmt == "e4m3":
        vals = words.view(ml_dtypes.float8_e4m3fn).astype(np.float64)
    else:
        nib = np.empty((g, 128, n, 4), np.uint8)
        nib[..., 0::2] = words & 0xF
        nib[..., 1::2] = words >> 4
        vals = E2M1[nib]
    vals = vals * np.repeat(np.exp2(scales.astype(np.float64) - 127.0), 8, axis=1)[..., None]
    return vals.transpose(0, 1, 3, 2).reshape(g * 512, n)


def gelu(v):
    return 0.5 * v * (1.0 + np.tanh(np.sqrt(2.0 / np.pi) * (v + 0.044715 * v**3)))


def striped8(idx):
    return np.concatenate([v.reshape(-1, 16).T for v in idx]).astype(np.uint16)


def unstriped8(offs):
    return np.stack([offs[16 * g:16 * g + 16].T.reshape(-1) for g in range(8)]).astype(np.int64)


def heads(xT, wgt, idx8):
    k = np.arange(xT.shape[0])
    return wgt[k // 4 % 128] * xT[k[:, None], idx8[k % 512 // 64]]


K, D, H, N, T, S = 1024, 512, 1024, 512, 2048, 1024

def setup_inputs():
    n = np.random.standard_normal
    s, sx, u = mx_kscale(K)[:, None], mx_kscale(D)[:, None], mx_kscale(H)[:, None]
    tab_words, tab_scales = pack_weight(n((K, T)) * s, "e4m3")
    w4_words, w4_scales = pack_weight(n((H, N)) / np.sqrt(H) / u, "e2m1")
    return {
        "tab_words": tab_words, "tab_scales": tab_scales,
        "offs": striped(np.random.permutation(T)[:S]),
        "xT": (n((D, T)) * sx).astype(np.float32),
        "wgt": np.repeat(np.random.uniform(0.5, 2.0, (8, S)), 16, axis=0).astype(np.float32),
        "offs2": striped8(np.stack([np.random.permutation(T)[:S] for _ in range(8)])),
        "w1": (n((K, H)) / np.sqrt(K) / s * u.T).astype(np.float32),
        "wx": (n((D, H)) / np.sqrt(D) / sx * u.T).astype(np.float32),
        "b1": (0.3 * n(H) * u[:, 0]).astype(np.float32),
        "w4_words": w4_words, "w4_scales": w4_scales,
        "b2": (1.0 + 0.3 * n(N)).astype(np.float32),
        "wp": (n((D, N)) / np.sqrt(D) / sx).astype(np.float32),
    }

def reference(tab_words, tab_scales, offs, xT, wgt, offs2, w1, wx, b1, w4_words, w4_scales, b2, wp):
    v = unpack_weight(tab_words, tab_scales, "e4m3")[:, unstriped(offs)]
    xg = heads(f64(xT), f64(wgt), unstriped8(offs2))
    xq = mxq(xg, 0, "e4m3")
    w1q = mxq(f64(w1), 0, "e4m3")
    wxq = mxq(f64(wx), 0, "e4m3")
    wpq = mxq(f64(wp), 0, "e4m3")
    w4 = unpack_weight(w4_words, w4_scales, "e2m1")
    a = w1q.T @ v + wxq.T @ xq
    h = np.maximum(a + f64(b1)[:, None], 0.0)
    g = (w4.T @ mxq(h, 0, "e4m3")) + f64(b2)[:, None]
    p = wpq.T @ xq
    return g * p

@@ -1,0 +1,379 @@
+from contextlib import ExitStack
+
+import concourse.mybir as mybir
+
+K, D, H, N, T, S = 1024, 512, 1024, 512, 2048, 1024
+FLOPS = 2 * S * (K * H + D * H + H * N + D * N)
+
+F32 = mybir.dt.float32
+BF16 = mybir.dt.bfloat16
+I32 = mybir.dt.int32
+U32 = mybir.dt.uint32
+U16 = mybir.dt.uint16
+U8 = mybir.dt.uint8
+FP8X4 = mybir.dt.float8_e4m3fn_x4
+FP4X4 = mybir.dt.float4_e2m1fn_x4
+ALU = mybir.AluOpType
+ACT = mybir.ActivationFunctionType
+
+P = 128
+PACK = 4
+KP = P * PACK
+HALF = 512
+GROUPED_BUFS = 6
+STEPS = [
+    ("lwgt", 0),
+    ("lts", 0),
+    ("ls", "x_lists"),
+    ("ls", "tab_list"),
+    ("lwgt", 1),
+    ("lx", 0),
+    ("lx", 3),
+    ("lx", 2),
+    ("gx", 0, 0),
+    ("lts", 2),
+    ("lx", 1),
+    ("lts", 3),
+    ("gx", 1, 0),
+    ("gx", 3, 0),
+    ("gx", 0, 1),
+    ("lw", "wp"),
+    ("lts", 1),
+    ("gx", 1, 1),
+    ("lw", "w02"),
+    ("cast", "wp", 0, 4, "V"),
+    ("lw", "w00"),
+    ("cast", "w02", 0, 4, "S"),
+    ("lt", 0),
+    ("lt", 1),
+    ("gx", 2, 0),
+    ("gx", 3, 1),
+    ("cast", "w00", 0, 4, "S"),
+    ("gx", 2, 1),
+    ("lw", "w01"),
+    ("ls", "b1"),
+    ("cast", "w01", 0, 2, "V"),
+    ("cast", "w01", 2, 4, "S"),
+    ("cast", "xg0", 0, 4, "S"),
+    ("q", "wp", 0, 4),
+    ("q", "xg0", 0, 4),
+    ("cast", "xg1", 0, 1, "V"),
+    ("q", "w01", 0, 4),
+    ("lw", "w12"),
+    ("lw", "w10"),
+    ("p", 0, 0),
+    ("cast", "xg1", 1, 4, "S"),
+    ("gt", 1, 1),
+    ("p", 0, 1),
+    ("lw", "w11"),
+    ("cast", "w11", 0, 4, "V"),
+    ("gs", 1),
+    ("q", "xg1", 0, 4),
+    ("gt", 0, 0),
+    ("q", "w00", 0, 4),
+    ("pe", 0, 1, "S"),
+    ("pe", 0, 0, "S"),
+    ("l4s", 1),
+    ("p", 0, 3),
+    ("gs", 0),
+    ("q", "w02", 0, 4),
+    ("p", 0, 2),
+    ("pe", 0, 2, "S"),
+    ("gt", 1, 0),
+    ("pe", 0, 3, "S"),
+    ("l1", 0, 0, 2),
+    ("l1", 0, 1, 2),
+    ("cast", "w10", 0, 4, "V"),
+    ("l1", 0, 0, 0),
+    ("cast", "w12", 0, 4, "V"),
+    ("gt", 0, 1),
+    ("l1", 0, 0, 1),
+    ("l1", 0, 1, 0),
+    ("he", 0, 0, 1, 0, 4, "S"),
+    ("l1", 0, 1, 1),
+    ("he", 0, 1, 2, 2, 4, "S"),
+    ("he", 0, 1, 2, 0, 2, "S"),
+    ("q", "w11", 0, 4),
+    ("he", 0, 0, 2, 0, 4, "S"),
+    ("he", 0, 1, 1, 0, 2, "S"),
+    ("he", 0, 1, 1, 2, 4, "S"),
+    ("he", 0, 1, 3, 2, 4, "S"),
+    ("he", 0, 1, 0, 2, 4, "S"),
+    ("he", 0, 0, 3, 0, 4, "S"),
+    ("he", 0, 1, 3, 0, 2, "S"),
+    ("he", 0, 0, 0, 0, 4, "S"),
+    ("q", "w10", 0, 4),
+    ("he", 0, 1, 0, 0, 2, "S"),
+    ("q", "w12", 0, 4),
+    ("il", 0, 1, 2, 4, "S"),
+    ("l4s", 2),
+    ("l1", 1, 0, 2),
+    ("l1", 1, 1, 2),
+    ("l1", 1, 1, 0),
+    ("l1", 1, 0, 0),
+    ("l1", 1, 0, 1),
+    ("l1", 1, 1, 1),
+    ("he", 1, 1, 1, 0, 2, "S"),
+    ("ls", "w4"),
+    ("he", 1, 1, 0, 0, 2, "S"),
+    ("l4s", 3),
+    ("il", 0, 0, 0, 4, "V"),
+    ("q", "h00", 0, 4),
+    ("he", 1, 1, 1, 2, 4, "S"),
+    ("he", 1, 0, 3, 0, 4, "V"),
+    ("he", 1, 0, 1, 0, 4, "V"),
+    ("il", 0, 1, 0, 2, "S"),
+    ("he", 1, 1, 2, 2, 4, "S"),
+    ("ls", "b2"),
+    ("he", 1, 0, 0, 0, 4, "S"),
+    ("he", 1, 1, 2, 0, 2, "S"),
+    ("he", 1, 0, 2, 0, 4, "S"),
+    ("il", 1, 0, 0, 4, "V"),
+    ("l4s", 0),
+    ("he", 1, 1, 3, 2, 4, "S"),
+    ("q", "h10", 0, 4),
+    ("he", 1, 1, 0, 2, 4, "S"),
+    ("p", 1, 0),
+    ("p", 1, 1),
+    ("g", 0, 0),
+    ("p", 1, 2),
+    ("he", 1, 1, 3, 0, 2, "S"),
+    ("il", 1, 1, 0, 2, "V"),
+    ("q", "h01", 2, 4),
+    ("p", 1, 3),
+    ("pe", 1, 3, "S"),
+    ("g", 0, 1),
+    ("q", "h11", 0, 2),
+    ("il", 1, 1, 2, 4, "S"),
+    ("f", 0, 1),
+    ("q", "h11", 2, 4),
+    ("f", 0, 0),
+    ("pe", 1, 0, "S"),
+    ("pe", 1, 2, "S"),
+    ("q", "h01", 0, 2),
+    ("pe", 1, 1, "S"),
+    ("g", 1, 0),
+    ("f", 0, 3),
+    ("g", 1, 1),
+    ("f", 0, 2),
+    ("f", 1, 0),
+    ("f", 1, 1),
+    ("f", 1, 3),
+    ("f", 1, 2),
+]
+
+
+def tile_list_contact_joint_gain_kernel(
+    tc, tab_words, tab_scales, offs, xT, wgt, offs2, w1, wx, b1, w4_words, w4_scales, b2, wp, out
+):
+    nc = tc.nc
+    with ExitStack() as ctx:
+        lists = ctx.enter_context(tc.tile_pool(name="lists", bufs=1))
+        keep = ctx.enter_context(tc.tile_pool(name="keep", bufs=1))
+        psum = ctx.enter_context(tc.psum_pool(name="psum", bufs=1))
+
+        tab_list = lists.tile([P, S // 16], U16, name="tab_list")
+        x_lists = lists.tile([P, S // 16], U16, name="x_lists")
+
+        x_plane = [keep.tile([P, T], F32, name=f"x_plane{i}", align_bytes=64) for i in range(PACK)]
+        wgt_sb = keep.tile([P, S], F32, name="wgt_sb", align_bytes=64)
+        tab_w = [keep.tile([P, T], I32, name=f"tab_w{a}", align_bytes=64) for a in range(2)]
+        tab_s = keep.tile([P, T // 4], I32, name="tab_s", align_bytes=64)
+        v_words = [keep.tile([P, S], U32, name=f"v_words{a}", align_bytes=64) for a in range(2)]
+        v_scales = keep.tile([P, S], U8, name="v_scales", align_bytes=64)
+        xg = [keep.tile([P, PACK, HALF], F32, name=f"xg{h}", align_bytes=64) for h in range(2)]
+        w4_w = keep.tile([P, 2, 2 * N], U8, name="w4_w", align_bytes=64)
+        w4_s = keep.tile([P, 2, N // 4], I32, name="w4_s", align_bytes=64)
+        b1_sb = keep.tile([P, 2, PACK], F32, name="b1_sb", align_bytes=64)
+        b2_sb = keep.tile([P, 4], F32, name="b2_sb", align_bytes=64)
+        p_sb = keep.tile([P, 2, 4, HALF], F32, name="p_sb", align_bytes=64)
+        warm_in = keep.tile([P, 8], F32, name="warm_in", align_bytes=64)
+        warm_out = keep.tile([P, 8], F32, name="warm_out", align_bytes=64)
+
+        names = ["xg0", "xg1", "wp", "w00", "w01", "w02", "w10", "w11", "w12", "h00", "h01", "h10", "h11"]
+        codes = {n: keep.tile([P, HALF], U32, name=f"codes_{n}", align_bytes=64) for n in names}
+        scales = {n: keep.tile([P, HALF], U8, name=f"scales_{n}", align_bytes=64) for n in names}
+        raw = {n: keep.tile([P, PACK, HALF], F32, name=f"raw_{n}", align_bytes=64) for n in names if n[0] == "w"}
+        grouped_ring = [keep.tile([P, PACK * HALF], BF16, name=f"grouped{n}", align_bytes=64) for n in range(GROUPED_BUFS)]
+        planes_ring = [keep.tile([P, PACK, HALF], BF16, name=f"planes{n}", align_bytes=64) for n in range(3)]
+        bank_tiles = {(h, i): psum.tile([P, HALF], F32, name=f"bank{h}{i}") for h in range(2) for i in range(4)}
+
+        def cols(h):
+            return slice(HALF * h, HALF * (h + 1))
+
+        def load_x(i):
+            nc.sync.dma_start(out=x_plane[i][:], in_=xT.rearrange("(p i) t -> p i t", i=PACK)[:, i, :])
+
+        def load_wgt(h):
+            nc.sync.dma_start(out=wgt_sb[:, cols(h)], in_=wgt[:, cols(h)])
+
+        def load_tab(a):
+            nc.sync.dma_start(out=tab_w[a][:], in_=tab_words[a].rearrange("p t i -> p (t i)").bitcast(I32))
+
+        def load_tab_scales(q):
+            nc.sync.dma_start(out=tab_s[32 * q : 32 * q + 8, :], in_=tab_scales[:, 4 * q : 4 * q + 4, :].bitcast(I32))
+
+        def load_w4_scales(q):
+            nc.sync.dma_start(
+                out=w4_s[32 * q : 32 * q + 4, :, :],
+                in_=w4_scales[:, 4 * q : 4 * q + 4, :].bitcast(I32).rearrange("a r c -> r a c"),
+            )
+
+        def load_weight(name):
+            if name == "wp":
+                src = wp
+            else:
+                b, a = int(name[1]), int(name[2])
+                src = wx[:, cols(b)] if a == 2 else w1[KP * a : KP * (a + 1), cols(b)]
+            nc.sync.dma_start(out=raw[name][:], in_=src.rearrange("(p j) c -> p j c", j=PACK))
+
+        def quantize(name, q0, q1):
+            c0, c1 = P * q0, P * q1
+            nc.vector.quantize_mx(
+                out=codes[name][:, c0:c1].bitcast(FP8X4),
+                scales=scales[name][:, c0:c1],
+                in_=grouped[name][:, PACK * c0 : PACK * c1],
+            )
+
+        grouped = {}
+
+        def new_grouped(name):
+            if name not in grouped:
+                grouped[name] = grouped_ring[len(grouped) % GROUPED_BUFS]
+            return grouped[name]
+
+        def copy_on(eng, dst, src):
+            if eng == "S":
+                nc.scalar.copy(out=dst, in_=src)
+            else:
+                nc.vector.tensor_copy(out=dst, in_=src)
+
+        def cast(name, q0, q1, eng):
+            dst = new_grouped(name)
+            if name in ("wp", "xg0", "xg1"):
+                src = raw[name] if name == "wp" else xg[int(name[2])]
+                c = slice(32 * q0, 32 * q1)
+                copy_on(
+                    eng,
+                    dst[:].rearrange("p (c i j) -> p c j i", i=4, j=PACK)[:, c],
+                    src[:].rearrange("p j (c i) -> p c j i", i=4)[:, c],
+                )
+            else:
+                copy_on(
+                    eng,
+                    dst[:].rearrange("p (t m j) -> p m j t", t=PACK, j=PACK)[:, :, :, q0:q1],
+                    raw[name][:].rearrange("p j (m t) -> p m j t", t=PACK)[:, :, :, q0:q1],
+                )
+
+        def gather_x(i, h):
+            nc.vector.tensor_tensor(
+                xg[h][:, i, :], x_plane[i][:].indirect(x_lists[:, 32 * h : 32 * (h + 1)]), wgt_sb[:, cols(h)], ALU.mult
+            )
+
+        def gather_words(a, h):
+            nc.vector.tensor_copy(
+                v_words[a][:, cols(h)], tab_w[a][:].bitcast(U32).indirect(tab_list[:, 32 * h : 32 * (h + 1)])
+            )
+
+        def gather_scales(h):
+            nc.vector.tensor_copy(
+                v_scales[:, cols(h)], tab_s[:].bitcast(U8).indirect(tab_list[:, 32 * h : 32 * (h + 1)])
+            )
+
+        def bank(h, i):
+            return bank_tiles[h, i]
+
+        def stationary(name, i):
+            c = slice(P * i, P * (i + 1))
+            return codes[name][:, c].bitcast(FP8X4), scales[name][:, c]
+
+        def moving(a, h):
+            if a == 2:
+                return codes[f"xg{h}"][:].bitcast(FP8X4), scales[f"xg{h}"][:]
+            return v_words[a][:, cols(h)].bitcast(FP8X4), v_scales[4 * a : P, cols(h)]
+
+        def mm(acc, st, mv, start, stop):
+            nc.tensor.matmul_mx(
+                out=acc[:], lhsT=st[0], lhsT_scale=st[1], rhs=mv[0], rhs_scale=mv[1], start=start, stop=stop
+            )
+
+        banks = {}
+        planes = {}
+        passes_done = {}
+
+        def projection(h, i):
+            banks[h, i] = bank(h, i)
+            mm(banks[h, i], stationary("wp", i), moving(2, h), True, True)
+
+        def keep_projection(h, i, eng):
+            copy_on(eng, p_sb[:, h, i, :], banks[h, i][:])
+
+        def layer1_pass(b, h, a):
+            n = passes_done.get((b, h), 0)
+            passes_done[b, h] = n + 1
+            for t in range(PACK):
+                if n == 0:
+                    banks[h, t] = bank(h, t)
+                mm(banks[h, t], stationary(f"w{b}{a}", t), moving(a, h), n == 0, n == 2)
+
+        def relu(b, h, t, q0, q1, eng):
+            if (b, h) not in planes:
+                planes[b, h] = planes_ring[len(planes) % 3]
+            c = slice(P * q0, P * q1)
+            if eng == "S":
+                nc.scalar.activation(out=planes[b, h][:, t, c], in_=banks[h, t][:, c], func=ACT.Relu, bias=b1_sb[:, b, t : t + 1])
+            else:
+                nc.vector.tensor_scalar(planes[b, h][:, t, c], banks[h, t][:, c], b1_sb[:, b, t : t + 1], 0.0, ALU.add, ALU.max)
+
+        def interleave(b, h, q0, q1, eng):
+            dst = new_grouped(f"h{b}{h}")
+            c = slice(32 * q0, 32 * q1)
+            copy_on(
+                eng,
+                dst[:].rearrange("p (c i j) -> p c j i", i=4, j=PACK)[:, c],
+                planes[b, h][:].rearrange("p j (c i) -> p c j i", i=4)[:, c],
+            )
+
+        def gain_pass(h, b):
+            for i in range(4):
+                if b == 0:
+                    banks[h, i] = bank(h, i)
+                st = (
+                    w4_w[:, b, 2 * P * i : 2 * P * (i + 1)].bitcast(FP4X4),
+                    w4_s[:, b, 32 * i : 32 * (i + 1)].bitcast(U8),
+                )
+                mm(banks[h, i], st, (codes[f"h{b}{h}"][:].bitcast(FP8X4), scales[f"h{b}{h}"][:]), b == 0, b == 1)
+
+        def finish(h, i):
+            res = p_sb[:, h, i, :]
+            nc.vector.scalar_tensor_tensor(
+                out=res, in0=banks[h, i][:], scalar=b2_sb[:, i : i + 1], in1=res, op0=ALU.add, op1=ALU.mult
+            )
+            nc.sync.dma_start(out=out[P * i : P * (i + 1), cols(h)], in_=res)
+
+        def load_small(what):
+            if what == "x_lists":
+                nc.sync.dma_start(x_lists[:], offs2)
+            elif what == "tab_list":
+                nc.sync.dma_start(tab_list[:], offs)
+            elif what == "b1":
+                nc.sync.dma_start(out=b1_sb[:], in_=b1.rearrange("(b p t) -> p b t", p=P, t=PACK))
+            elif what == "w4":
+                nc.sync.dma_start(out=w4_w[:].bitcast(I32), in_=w4_words.rearrange("a p c -> p a c").bitcast(I32))
+            else:
+                with nc.allow_non_contiguous_dma(reason="one bias value a partition"):
+                    nc.sync.dma_start(out=b2_sb[:], in_=b2.rearrange("(i p) -> p i", p=P))
+
+        nc.vector.memset(tab_s[:], 0)
+        nc.vector.memset(warm_in[:], 0.0)
+        nc.vector.memset(w4_s[:], 0)
+        nc.scalar.activation(out=warm_out[:], in_=warm_in[:], func=ACT.Relu)
+
+        do = {
+            "lx": load_x, "lwgt": load_wgt, "lt": load_tab, "lts": load_tab_scales, "l4s": load_w4_scales,
+            "lw": load_weight, "ls": load_small, "gx": gather_x, "gt": gather_words, "gs": gather_scales,
+            "cast": cast, "q": quantize, "p": projection, "pe": keep_projection, "l1": layer1_pass, "he": relu,
+            "il": interleave, "g": gain_pass, "f": finish,
+        }
+        for step in STEPS:
+            do[step[0]](*step[1:])

@@ -18,149 +18,27 @@ ACT = mybir.ActivationFunctionType
 
 P = 128
 PACK = 4
-KP = P * PACK
-HALF = 512
-GROUPED_BUFS = 6
-STEPS = [
-    ("lwgt", 0),
-    ("lts", 0),
-    ("ls", "x_lists"),
-    ("ls", "tab_list"),
-    ("lwgt", 1),
-    ("lx", 0),
-    ("lx", 3),
-    ("lx", 2),
-    ("gx", 0, 0),
-    ("lts", 2),
-    ("lx", 1),
-    ("lts", 3),
-    ("gx", 1, 0),
-    ("gx", 3, 0),
-    ("gx", 0, 1),
-    ("lw", "wp"),
-    ("lts", 1),
-    ("gx", 1, 1),
-    ("lw", "w02"),
-    ("cast", "wp", 0, 4, "V"),
-    ("lw", "w00"),
-    ("cast", "w02", 0, 4, "S"),
-    ("lt", 0),
-    ("lt", 1),
-    ("gx", 2, 0),
-    ("gx", 3, 1),
-    ("cast", "w00", 0, 4, "S"),
-    ("gx", 2, 1),
-    ("lw", "w01"),
-    ("ls", "b1"),
-    ("cast", "w01", 0, 2, "V"),
-    ("cast", "w01", 2, 4, "S"),
-    ("cast", "xg0", 0, 4, "S"),
-    ("q", "wp", 0, 4),
-    ("q", "xg0", 0, 4),
-    ("cast", "xg1", 0, 1, "V"),
-    ("q", "w01", 0, 4),
-    ("lw", "w12"),
-    ("lw", "w10"),
-    ("p", 0, 0),
-    ("cast", "xg1", 1, 4, "S"),
-    ("gt", 1, 1),
-    ("p", 0, 1),
-    ("lw", "w11"),
-    ("cast", "w11", 0, 4, "V"),
-    ("gs", 1),
-    ("q", "xg1", 0, 4),
-    ("gt", 0, 0),
-    ("q", "w00", 0, 4),
-    ("pe", 0, 1, "S"),
-    ("pe", 0, 0, "S"),
-    ("l4s", 1),
-    ("p", 0, 3),
-    ("gs", 0),
-    ("q", "w02", 0, 4),
-    ("p", 0, 2),
-    ("pe", 0, 2, "S"),
-    ("gt", 1, 0),
-    ("pe", 0, 3, "S"),
-    ("l1", 0, 0, 2),
-    ("l1", 0, 1, 2),
-    ("cast", "w10", 0, 4, "V"),
-    ("l1", 0, 0, 0),
-    ("cast", "w12", 0, 4, "V"),
-    ("gt", 0, 1),
-    ("l1", 0, 0, 1),
-    ("l1", 0, 1, 0),
-    ("he", 0, 0, 1, 0, 4, "S"),
-    ("l1", 0, 1, 1),
-    ("he", 0, 1, 2, 2, 4, "S"),
-    ("he", 0, 1, 2, 0, 2, "S"),
-    ("q", "w11", 0, 4),
-    ("he", 0, 0, 2, 0, 4, "S"),
-    ("he", 0, 1, 1, 0, 2, "S"),
-    ("he", 0, 1, 1, 2, 4, "S"),
-    ("he", 0, 1, 3, 2, 4, "S"),
-    ("he", 0, 1, 0, 2, 4, "S"),
-    ("he", 0, 0, 3, 0, 4, "S"),
-    ("he", 0, 1, 3, 0, 2, "S"),
-    ("he", 0, 0, 0, 0, 4, "S"),
-    ("q", "w10", 0, 4),
-    ("he", 0, 1, 0, 0, 2, "S"),
-    ("q", "w12", 0, 4),
-    ("il", 0, 1, 2, 4, "S"),
-    ("l4s", 2),
-    ("l1", 1, 0, 2),
-    ("l1", 1, 1, 2),
-    ("l1", 1, 1, 0),
-    ("l1", 1, 0, 0),
-    ("l1", 1, 0, 1),
-    ("l1", 1, 1, 1),
-    ("he", 1, 1, 1, 0, 2, "S"),
-    ("ls", "w4"),
-    ("he", 1, 1, 0, 0, 2, "S"),
-    ("l4s", 3),
-    ("il", 0, 0, 0, 4, "V"),
-    ("q", "h00", 0, 4),
-    ("he", 1, 1, 1, 2, 4, "S"),
-    ("he", 1, 0, 3, 0, 4, "V"),
-    ("he", 1, 0, 1, 0, 4, "V"),
-    ("il", 0, 1, 0, 2, "S"),
-    ("he", 1, 1, 2, 2, 4, "S"),
-    ("ls", "b2"),
-    ("he", 1, 0, 0, 0, 4, "S"),
-    ("he", 1, 1, 2, 0, 2, "S"),
-    ("he", 1, 0, 2, 0, 4, "S"),
-    ("il", 1, 0, 0, 4, "V"),
-    ("l4s", 0),
-    ("he", 1, 1, 3, 2, 4, "S"),
-    ("q", "h10", 0, 4),
-    ("he", 1, 1, 0, 2, 4, "S"),
-    ("p", 1, 0),
-    ("p", 1, 1),
-    ("g", 0, 0),
-    ("p", 1, 2),
-    ("he", 1, 1, 3, 0, 2, "S"),
-    ("il", 1, 1, 0, 2, "V"),
-    ("q", "h01", 2, 4),
-    ("p", 1, 3),
-    ("pe", 1, 3, "S"),
-    ("g", 0, 1),
-    ("q", "h11", 0, 2),
-    ("il", 1, 1, 2, 4, "S"),
-    ("f", 0, 1),
-    ("q", "h11", 2, 4),
-    ("f", 0, 0),
-    ("pe", 1, 0, "S"),
-    ("pe", 1, 2, "S"),
-    ("q", "h01", 0, 2),
-    ("pe", 1, 1, "S"),
-    ("g", 1, 0),
-    ("f", 0, 3),
-    ("g", 1, 1),
-    ("f", 0, 2),
-    ("f", 1, 0),
-    ("f", 1, 1),
-    ("f", 1, 3),
-    ("f", 1, 2),
-]
+K_PASS = P * PACK
+WIDTH = 512
+TILES = WIDTH // P
+LIST_COLS = WIDTH // 16
+QUADRANT = 32
+
+SCALAR, VECTOR = "scalar", "vector"
+
+WHOLE, FIRST, SECOND, QUARTER, REST = (0, 4), (0, 2), (2, 4), (0, 1), (1, 4)
+
+OPERANDS = ("xg_0", "xg_1", "wp", "w1lo_0", "w1hi_0", "wx_0", "w1lo_1", "w1hi_1", "wx_1",
+            "hid_0_0", "hid_0_1", "hid_1_0", "hid_1_1")
+STAGING = (
+    ("wx_0", "w1hi_1", "hid_1_1"),
+    ("xg_1", "w1lo_1"),
+    ("w1hi_0",),
+    ("xg_0", "hid_0_0"),
+    ("w1lo_0", "wp", "hid_1_0"),
+    ("wx_1", "hid_0_1"),
+)
+RELU_BUFFER = {(0, 0): 2, (0, 1): 0, (1, 0): 1, (1, 1): 2}
 
 
 def tile_list_contact_joint_gain_kernel(
@@ -175,205 +53,322 @@ def tile_list_contact_joint_gain_kernel(
         tab_list = lists.tile([P, S // 16], U16, name="tab_list")
         x_lists = lists.tile([P, S // 16], U16, name="x_lists")
 
-        x_plane = [keep.tile([P, T], F32, name=f"x_plane{i}", align_bytes=64) for i in range(PACK)]
+        x_plane = [keep.tile([P, T], F32, name=f"x_plane{j}", align_bytes=64) for j in range(PACK)]
         wgt_sb = keep.tile([P, S], F32, name="wgt_sb", align_bytes=64)
         tab_w = [keep.tile([P, T], I32, name=f"tab_w{a}", align_bytes=64) for a in range(2)]
         tab_s = keep.tile([P, T // 4], I32, name="tab_s", align_bytes=64)
         v_words = [keep.tile([P, S], U32, name=f"v_words{a}", align_bytes=64) for a in range(2)]
         v_scales = keep.tile([P, S], U8, name="v_scales", align_bytes=64)
-        xg = [keep.tile([P, PACK, HALF], F32, name=f"xg{h}", align_bytes=64) for h in range(2)]
+        xg = [keep.tile([P, PACK, WIDTH], F32, name=f"xg{h}", align_bytes=64) for h in range(2)]
         w4_w = keep.tile([P, 2, 2 * N], U8, name="w4_w", align_bytes=64)
         w4_s = keep.tile([P, 2, N // 4], I32, name="w4_s", align_bytes=64)
         b1_sb = keep.tile([P, 2, PACK], F32, name="b1_sb", align_bytes=64)
-        b2_sb = keep.tile([P, 4], F32, name="b2_sb", align_bytes=64)
-        p_sb = keep.tile([P, 2, 4, HALF], F32, name="p_sb", align_bytes=64)
-        warm_in = keep.tile([P, 8], F32, name="warm_in", align_bytes=64)
-        warm_out = keep.tile([P, 8], F32, name="warm_out", align_bytes=64)
+        b2_sb = keep.tile([P, TILES], F32, name="b2_sb", align_bytes=64)
+        result = keep.tile([P, 2, TILES, WIDTH], F32, name="result", align_bytes=64)
 
-        names = ["xg0", "xg1", "wp", "w00", "w01", "w02", "w10", "w11", "w12", "h00", "h01", "h10", "h11"]
-        codes = {n: keep.tile([P, HALF], U32, name=f"codes_{n}", align_bytes=64) for n in names}
-        scales = {n: keep.tile([P, HALF], U8, name=f"scales_{n}", align_bytes=64) for n in names}
-        raw = {n: keep.tile([P, PACK, HALF], F32, name=f"raw_{n}", align_bytes=64) for n in names if n[0] == "w"}
-        grouped_ring = [keep.tile([P, PACK * HALF], BF16, name=f"grouped{n}", align_bytes=64) for n in range(GROUPED_BUFS)]
-        planes_ring = [keep.tile([P, PACK, HALF], BF16, name=f"planes{n}", align_bytes=64) for n in range(3)]
-        bank_tiles = {(h, i): psum.tile([P, HALF], F32, name=f"bank{h}{i}") for h in range(2) for i in range(4)}
+        codes = {n: keep.tile([P, WIDTH], U32, name=f"codes_{n}", align_bytes=64) for n in OPERANDS}
+        scales = {n: keep.tile([P, WIDTH], U8, name=f"scales_{n}", align_bytes=64) for n in OPERANDS}
+        raw = {n: keep.tile([P, PACK, WIDTH], F32, name=f"raw_{n}", align_bytes=64) for n in OPERANDS if n[0] == "w"}
+        raw["xg_0"], raw["xg_1"] = xg
+        staged = {}
+        for slot, users in enumerate(STAGING):
+            buffer = keep.tile([P, PACK * WIDTH], BF16, name=f"staging{slot}", align_bytes=64)
+            for n in users:
+                staged[n] = buffer
+        relu_buffers = [keep.tile([P, PACK, WIDTH], BF16, name=f"relu{slot}", align_bytes=64) for slot in range(3)]
+        banks = {(h, t): psum.tile([P, WIDTH], F32, name=f"bank{h}{t}") for h in range(2) for t in range(TILES)}
 
-        def cols(h):
-            return slice(HALF * h, HALF * (h + 1))
+        def span(i):
+            return slice(WIDTH * i, WIDTH * (i + 1))
 
-        def load_x(i):
-            nc.sync.dma_start(out=x_plane[i][:], in_=xT.rearrange("(p i) t -> p i t", i=PACK)[:, i, :])
+        def load_x(j):
+            nc.sync.dma_start(out=x_plane[j][:], in_=xT.rearrange("(p j) t -> p j t", j=PACK)[:, j, :])
 
         def load_wgt(h):
-            nc.sync.dma_start(out=wgt_sb[:, cols(h)], in_=wgt[:, cols(h)])
+            nc.sync.dma_start(out=wgt_sb[:, span(h)], in_=wgt[:, span(h)])
 
-        def load_tab(a):
-            nc.sync.dma_start(out=tab_w[a][:], in_=tab_words[a].rearrange("p t i -> p (t i)").bitcast(I32))
+        def load_table_words(a):
+            nc.sync.dma_start(out=tab_w[a][:], in_=tab_words[a].rearrange("p t j -> p (t j)").bitcast(I32))
 
-        def load_tab_scales(q):
-            nc.sync.dma_start(out=tab_s[32 * q : 32 * q + 8, :], in_=tab_scales[:, 4 * q : 4 * q + 4, :].bitcast(I32))
+        def load_table_scales(q):
+            rows = slice(QUADRANT * q, QUADRANT * q + 8)
+            nc.sync.dma_start(out=tab_s[rows, :], in_=tab_scales[:, 4 * q : 4 * q + 4, :].bitcast(I32))
+
+        def load_w4_words():
+            nc.sync.dma_start(out=w4_w[:].bitcast(I32), in_=w4_words.rearrange("b p c -> p b c").bitcast(I32))
 
         def load_w4_scales(q):
             nc.sync.dma_start(
-                out=w4_s[32 * q : 32 * q + 4, :, :],
-                in_=w4_scales[:, 4 * q : 4 * q + 4, :].bitcast(I32).rearrange("a r c -> r a c"),
+                out=w4_s[QUADRANT * q : QUADRANT * q + 4, :, :],
+                in_=w4_scales[:, 4 * q : 4 * q + 4, :].bitcast(I32).rearrange("b r c -> r b c"),
             )
 
-        def load_weight(name):
-            if name == "wp":
-                src = wp
-            else:
-                b, a = int(name[1]), int(name[2])
-                src = wx[:, cols(b)] if a == 2 else w1[KP * a : KP * (a + 1), cols(b)]
-            nc.sync.dma_start(out=raw[name][:], in_=src.rearrange("(p j) c -> p j c", j=PACK))
+        def load_b1():
+            nc.sync.dma_start(out=b1_sb[:], in_=b1.rearrange("(b p t) -> p b t", p=P, t=PACK))
 
-        def quantize(name, q0, q1):
-            c0, c1 = P * q0, P * q1
+        def load_b2():
+            with nc.allow_non_contiguous_dma(reason="one bias value for each partition and output tile"):
+                nc.sync.dma_start(out=b2_sb[:], in_=b2.rearrange("(t p) -> p t", p=P))
+
+        weight_rows = {"wp": wp}
+        for b in range(2):
+            weight_rows[f"wx_{b}"] = wx[:, span(b)]
+            weight_rows[f"w1lo_{b}"] = w1[:K_PASS, span(b)]
+            weight_rows[f"w1hi_{b}"] = w1[K_PASS:, span(b)]
+
+        def load_weight(name):
+            nc.sync.dma_start(out=raw[name][:], in_=weight_rows[name].rearrange("(p j) c -> p j c", j=PACK))
+
+        def gather_x(j, h):
+            picked = x_plane[j][:].indirect(x_lists[:, LIST_COLS * h : LIST_COLS * (h + 1)])
+            nc.vector.tensor_tensor(xg[h][:, j, :], picked, wgt_sb[:, span(h)], ALU.mult)
+
+        def gather_words(a, h):
+            picked = tab_w[a][:].bitcast(U32).indirect(tab_list[:, LIST_COLS * h : LIST_COLS * (h + 1)])
+            nc.vector.tensor_copy(v_words[a][:, span(h)], picked)
+
+        def gather_scales(h):
+            picked = tab_s[:].bitcast(U8).indirect(tab_list[:, LIST_COLS * h : LIST_COLS * (h + 1)])
+            nc.vector.tensor_copy(v_scales[:, span(h)], picked)
+
+        def round_to_bf16(engine, dst, src):
+            if engine == SCALAR:
+                nc.scalar.activation(out=dst, in_=src, func=ACT.Copy)
+            else:
+                nc.vector.tensor_copy(out=dst, in_=src)
+
+        def side_by_side(name, rows, part):
+            groups = slice(part[0] * P // 4, part[1] * P // 4)
+            dst = staged[name][:].rearrange("p (g i j) -> p g j i", i=4, j=PACK)[:, groups]
+            return dst, rows[:].rearrange("p j (g i) -> p g j i", i=4)[:, groups]
+
+        def round_columns(name, part, engine):
+            round_to_bf16(engine, *side_by_side(name, raw[name], part))
+
+        def round_tiles(name, part, engine):
+            round_to_bf16(
+                engine,
+                staged[name][:].rearrange("p (t m j) -> p m j t", t=TILES, j=PACK)[:, :, :, part[0] : part[1]],
+                raw[name][:].rearrange("p j (m t) -> p m j t", t=TILES)[:, :, :, part[0] : part[1]],
+            )
+
+        def quantize(name, part):
+            c0, c1 = P * part[0], P * part[1]
             nc.vector.quantize_mx(
                 out=codes[name][:, c0:c1].bitcast(FP8X4),
                 scales=scales[name][:, c0:c1],
-                in_=grouped[name][:, PACK * c0 : PACK * c1],
+                in_=staged[name][:, PACK * c0 : PACK * c1],
             )
 
-        grouped = {}
+        def tile_of(name, t):
+            c = slice(P * t, P * (t + 1))
+            return codes[name][:, c].bitcast(FP8X4), scales[name][:, c]
 
-        def new_grouped(name):
-            if name not in grouped:
-                grouped[name] = grouped_ring[len(grouped) % GROUPED_BUFS]
-            return grouped[name]
+        def all_columns(name):
+            return codes[name][:].bitcast(FP8X4), scales[name][:]
 
-        def copy_on(eng, dst, src):
-            if eng == "S":
+        def table_pass(a, h):
+            return v_words[a][:, span(h)].bitcast(FP8X4), v_scales[4 * a : P, span(h)]
+
+        def multiply(bank, stationary, moving, start, stop):
+            nc.tensor.matmul_mx(
+                out=bank[:], lhsT=stationary[0], lhsT_scale=stationary[1], rhs=moving[0], rhs_scale=moving[1],
+                start=start, stop=stop,
+            )
+
+        def hidden_pass(weight, b, h):
+            moving = {"wx": all_columns(f"xg_{h}"), "w1lo": table_pass(0, h), "w1hi": table_pass(1, h)}[weight]
+            for t in range(TILES):
+                multiply(banks[h, t], tile_of(f"{weight}_{b}", t), moving, weight == "wx", weight == "w1hi")
+
+        def relu(b, h, t, part, engine):
+            c = slice(P * part[0], P * part[1])
+            dst = relu_buffers[RELU_BUFFER[b, h]][:, t, c]
+            bias = b1_sb[:, b, t : t + 1]
+            if engine == SCALAR:
+                nc.scalar.activation(out=dst, in_=banks[h, t][:, c], func=ACT.Relu, bias=bias)
+            else:
+                nc.vector.tensor_scalar(dst, banks[h, t][:, c], bias, 0.0, ALU.add, ALU.max)
+
+        def interleave(b, h, part, engine):
+            dst, src = side_by_side(f"hid_{b}_{h}", relu_buffers[RELU_BUFFER[b, h]], part)
+            if engine == SCALAR:
                 nc.scalar.copy(out=dst, in_=src)
             else:
                 nc.vector.tensor_copy(out=dst, in_=src)
 
-        def cast(name, q0, q1, eng):
-            dst = new_grouped(name)
-            if name in ("wp", "xg0", "xg1"):
-                src = raw[name] if name == "wp" else xg[int(name[2])]
-                c = slice(32 * q0, 32 * q1)
-                copy_on(
-                    eng,
-                    dst[:].rearrange("p (c i j) -> p c j i", i=4, j=PACK)[:, c],
-                    src[:].rearrange("p j (c i) -> p c j i", i=4)[:, c],
+        def project(h, t):
+            multiply(banks[h, t], tile_of("wp", t), all_columns(f"xg_{h}"), True, True)
+
+        def keep_projection(h, t):
+            nc.scalar.copy(out=result[:, h, t, :], in_=banks[h, t][:])
+
+        def gain_pass(b, h):
+            for t in range(TILES):
+                w4_tile = (
+                    w4_w[:, b, 2 * P * t : 2 * P * (t + 1)].bitcast(FP4X4),
+                    w4_s[:, b, P // 4 * t : P // 4 * (t + 1)].bitcast(U8),
                 )
-            else:
-                copy_on(
-                    eng,
-                    dst[:].rearrange("p (t m j) -> p m j t", t=PACK, j=PACK)[:, :, :, q0:q1],
-                    raw[name][:].rearrange("p j (m t) -> p m j t", t=PACK)[:, :, :, q0:q1],
-                )
+                multiply(banks[h, t], w4_tile, all_columns(f"hid_{b}_{h}"), b == 0, b == 1)
 
-        def gather_x(i, h):
-            nc.vector.tensor_tensor(
-                xg[h][:, i, :], x_plane[i][:].indirect(x_lists[:, 32 * h : 32 * (h + 1)]), wgt_sb[:, cols(h)], ALU.mult
-            )
-
-        def gather_words(a, h):
-            nc.vector.tensor_copy(
-                v_words[a][:, cols(h)], tab_w[a][:].bitcast(U32).indirect(tab_list[:, 32 * h : 32 * (h + 1)])
-            )
-
-        def gather_scales(h):
-            nc.vector.tensor_copy(
-                v_scales[:, cols(h)], tab_s[:].bitcast(U8).indirect(tab_list[:, 32 * h : 32 * (h + 1)])
-            )
-
-        def bank(h, i):
-            return bank_tiles[h, i]
-
-        def stationary(name, i):
-            c = slice(P * i, P * (i + 1))
-            return codes[name][:, c].bitcast(FP8X4), scales[name][:, c]
-
-        def moving(a, h):
-            if a == 2:
-                return codes[f"xg{h}"][:].bitcast(FP8X4), scales[f"xg{h}"][:]
-            return v_words[a][:, cols(h)].bitcast(FP8X4), v_scales[4 * a : P, cols(h)]
-
-        def mm(acc, st, mv, start, stop):
-            nc.tensor.matmul_mx(
-                out=acc[:], lhsT=st[0], lhsT_scale=st[1], rhs=mv[0], rhs_scale=mv[1], start=start, stop=stop
-            )
-
-        banks = {}
-        planes = {}
-        passes_done = {}
-
-        def projection(h, i):
-            banks[h, i] = bank(h, i)
-            mm(banks[h, i], stationary("wp", i), moving(2, h), True, True)
-
-        def keep_projection(h, i, eng):
-            copy_on(eng, p_sb[:, h, i, :], banks[h, i][:])
-
-        def layer1_pass(b, h, a):
-            n = passes_done.get((b, h), 0)
-            passes_done[b, h] = n + 1
-            for t in range(PACK):
-                if n == 0:
-                    banks[h, t] = bank(h, t)
-                mm(banks[h, t], stationary(f"w{b}{a}", t), moving(a, h), n == 0, n == 2)
-
-        def relu(b, h, t, q0, q1, eng):
-            if (b, h) not in planes:
-                planes[b, h] = planes_ring[len(planes) % 3]
-            c = slice(P * q0, P * q1)
-            if eng == "S":
-                nc.scalar.activation(out=planes[b, h][:, t, c], in_=banks[h, t][:, c], func=ACT.Relu, bias=b1_sb[:, b, t : t + 1])
-            else:
-                nc.vector.tensor_scalar(planes[b, h][:, t, c], banks[h, t][:, c], b1_sb[:, b, t : t + 1], 0.0, ALU.add, ALU.max)
-
-        def interleave(b, h, q0, q1, eng):
-            dst = new_grouped(f"h{b}{h}")
-            c = slice(32 * q0, 32 * q1)
-            copy_on(
-                eng,
-                dst[:].rearrange("p (c i j) -> p c j i", i=4, j=PACK)[:, c],
-                planes[b, h][:].rearrange("p j (c i) -> p c j i", i=4)[:, c],
-            )
-
-        def gain_pass(h, b):
-            for i in range(4):
-                if b == 0:
-                    banks[h, i] = bank(h, i)
-                st = (
-                    w4_w[:, b, 2 * P * i : 2 * P * (i + 1)].bitcast(FP4X4),
-                    w4_s[:, b, 32 * i : 32 * (i + 1)].bitcast(U8),
-                )
-                mm(banks[h, i], st, (codes[f"h{b}{h}"][:].bitcast(FP8X4), scales[f"h{b}{h}"][:]), b == 0, b == 1)
-
-        def finish(h, i):
-            res = p_sb[:, h, i, :]
+        def finish(h, t):
+            res = result[:, h, t, :]
             nc.vector.scalar_tensor_tensor(
-                out=res, in0=banks[h, i][:], scalar=b2_sb[:, i : i + 1], in1=res, op0=ALU.add, op1=ALU.mult
+                out=res, in0=banks[h, t][:], scalar=b2_sb[:, t : t + 1], in1=res, op0=ALU.add, op1=ALU.mult
             )
-            nc.sync.dma_start(out=out[P * i : P * (i + 1), cols(h)], in_=res)
-
-        def load_small(what):
-            if what == "x_lists":
-                nc.sync.dma_start(x_lists[:], offs2)
-            elif what == "tab_list":
-                nc.sync.dma_start(tab_list[:], offs)
-            elif what == "b1":
-                nc.sync.dma_start(out=b1_sb[:], in_=b1.rearrange("(b p t) -> p b t", p=P, t=PACK))
-            elif what == "w4":
-                nc.sync.dma_start(out=w4_w[:].bitcast(I32), in_=w4_words.rearrange("a p c -> p a c").bitcast(I32))
-            else:
-                with nc.allow_non_contiguous_dma(reason="one bias value a partition"):
-                    nc.sync.dma_start(out=b2_sb[:], in_=b2.rearrange("(i p) -> p i", p=P))
+            nc.sync.dma_start(out=out[P * t : P * (t + 1), span(h)], in_=res)
 
         nc.vector.memset(tab_s[:], 0)
-        nc.vector.memset(warm_in[:], 0.0)
         nc.vector.memset(w4_s[:], 0)
-        nc.scalar.activation(out=warm_out[:], in_=warm_in[:], func=ACT.Relu)
 
-        do = {
-            "lx": load_x, "lwgt": load_wgt, "lt": load_tab, "lts": load_tab_scales, "l4s": load_w4_scales,
-            "lw": load_weight, "ls": load_small, "gx": gather_x, "gt": gather_words, "gs": gather_scales,
-            "cast": cast, "q": quantize, "p": projection, "pe": keep_projection, "l1": layer1_pass, "he": relu,
-            "il": interleave, "g": gain_pass, "f": finish,
-        }
-        for step in STEPS:
-            do[step[0]](*step[1:])
+
+        load_wgt(1)
+        nc.sync.dma_start(x_lists[:], offs2)
+        load_x(0)
+        load_table_scales(0)
+        load_x(1)
+        load_wgt(0)
+        load_b1()
+        nc.sync.dma_start(tab_list[:], offs)
+        load_x(2)
+        load_x(3)
+        load_table_words(0)
+        load_weight("wx_0")
+        load_table_scales(1)
+        load_table_scales(2)
+        load_weight("w1lo_0")
+        load_table_scales(3)
+        load_table_words(1)
+        load_weight("w1hi_0")
+        load_weight("wx_1")
+        load_weight("w1lo_1")
+        load_weight("w1hi_1")
+        load_weight("wp")
+        load_w4_scales(0)
+        load_w4_scales(1)
+        load_w4_scales(2)
+        load_w4_words()
+        load_w4_scales(3)
+        load_b2()
+
+        gather_x(0, 1)
+        gather_x(1, 1)
+        gather_x(1, 0)
+        gather_x(0, 0)
+        gather_x(2, 1)
+        gather_x(2, 0)
+        gather_x(3, 1)
+        gather_x(3, 0)
+        round_columns("xg_1", FIRST, SCALAR)
+        round_columns("xg_0", QUARTER, VECTOR)
+        round_columns("xg_0", REST, SCALAR)
+        quantize("xg_1", FIRST)
+        gather_words(0, 0)
+        gather_words(0, 1)
+        round_columns("xg_1", SECOND, SCALAR)
+        quantize("xg_0", WHOLE)
+        quantize("xg_1", SECOND)
+
+        round_tiles("wx_0", FIRST, VECTOR)
+        round_tiles("wx_0", SECOND, VECTOR)
+        round_tiles("w1lo_0", WHOLE, SCALAR)
+        quantize("wx_0", FIRST)
+        quantize("wx_0", SECOND)
+        hidden_pass("wx", 0, 0)
+        gather_scales(0)
+        gather_scales(1)
+        hidden_pass("wx", 0, 1)
+        quantize("w1lo_0", WHOLE)
+        gather_words(1, 1)
+        hidden_pass("w1lo", 0, 1)
+        round_tiles("w1hi_0", SECOND, SCALAR)
+        gather_words(1, 0)
+        hidden_pass("w1lo", 0, 0)
+        round_tiles("w1hi_0", FIRST, SCALAR)
+        quantize("w1hi_0", FIRST)
+        quantize("w1hi_0", SECOND)
+
+        round_tiles("wx_1", FIRST, VECTOR)
+        round_tiles("wx_1", SECOND, SCALAR)
+        hidden_pass("w1hi", 0, 0)
+        relu(0, 0, 2, WHOLE, SCALAR)
+        relu(0, 0, 3, WHOLE, VECTOR)
+        hidden_pass("w1hi", 0, 1)
+        quantize("wx_1", FIRST)
+        relu(0, 0, 1, WHOLE, SCALAR)
+        quantize("wx_1", SECOND)
+        round_tiles("w1lo_1", FIRST, VECTOR)
+        relu(0, 0, 0, WHOLE, SCALAR)
+        relu(0, 1, 0, WHOLE, SCALAR)
+        round_tiles("w1lo_1", SECOND, VECTOR)
+        hidden_pass("wx", 1, 0)
+        relu(0, 1, 1, WHOLE, SCALAR)
+        interleave(0, 0, WHOLE, VECTOR)
+        relu(0, 1, 2, WHOLE, SCALAR)
+        relu(0, 1, 3, WHOLE, SCALAR)
+        hidden_pass("wx", 1, 1)
+        round_tiles("w1hi_1", FIRST, VECTOR)
+        interleave(0, 1, WHOLE, SCALAR)
+        quantize("w1lo_1", FIRST)
+        quantize("w1hi_1", FIRST)
+        quantize("hid_0_0", WHOLE)
+        round_tiles("w1hi_1", SECOND, VECTOR)
+        quantize("w1lo_1", SECOND)
+        hidden_pass("w1lo", 1, 0)
+        hidden_pass("w1lo", 1, 1)
+
+        round_columns("wp", REST, SCALAR)
+        round_columns("wp", QUARTER, VECTOR)
+        quantize("w1hi_1", SECOND)
+        hidden_pass("w1hi", 1, 0)
+        hidden_pass("w1hi", 1, 1)
+        relu(1, 0, 0, WHOLE, VECTOR)
+        relu(1, 0, 1, WHOLE, VECTOR)
+        relu(1, 1, 0, FIRST, SCALAR)
+        quantize("hid_0_1", WHOLE)
+        relu(1, 1, 1, SECOND, SCALAR)
+        relu(1, 1, 1, FIRST, SCALAR)
+        quantize("wp", WHOLE)
+        relu(1, 1, 0, SECOND, SCALAR)
+        relu(1, 0, 3, WHOLE, SCALAR)
+        relu(1, 0, 2, WHOLE, VECTOR)
+
+        project(0, 1)
+        project(0, 0)
+        relu(1, 1, 2, FIRST, SCALAR)
+        relu(1, 1, 3, SECOND, VECTOR)
+        project(0, 3)
+        interleave(1, 0, WHOLE, VECTOR)
+        relu(1, 1, 2, SECOND, SCALAR)
+        project(0, 2)
+        keep_projection(0, 1)
+        project(1, 1)
+        project(1, 0)
+        interleave(1, 1, SECOND, SCALAR)
+        project(1, 2)
+        relu(1, 1, 3, FIRST, VECTOR)
+        quantize("hid_1_0", WHOLE)
+        project(1, 3)
+        keep_projection(0, 3)
+        interleave(1, 1, FIRST, VECTOR)
+        keep_projection(0, 2)
+        quantize("hid_1_1", SECOND)
+        keep_projection(0, 0)
+        quantize("hid_1_1", FIRST)
+        keep_projection(1, 1)
+
+        gain_pass(0, 0)
+        keep_projection(1, 0)
+        gain_pass(1, 0)
+        finish(0, 1)
+        finish(0, 3)
+        finish(0, 2)
+        keep_projection(1, 3)
+        finish(0, 0)
+        keep_projection(1, 2)
+        gain_pass(0, 1)
+        gain_pass(1, 1)
+        finish(1, 1)
+        finish(1, 0)
+        finish(1, 3)
+        finish(1, 2)

from contextlib import ExitStack

import concourse.mybir as mybir

K, D, H, N, T, S = 1024, 512, 1024, 512, 2048, 1024
FLOPS = 2 * S * (K * H + D * H + H * N + D * N)

F32 = mybir.dt.float32
BF16 = mybir.dt.bfloat16
I32 = mybir.dt.int32
U32 = mybir.dt.uint32
U16 = mybir.dt.uint16
U8 = mybir.dt.uint8
FP8X4 = mybir.dt.float8_e4m3fn_x4
FP4X4 = mybir.dt.float4_e2m1fn_x4
ALU = mybir.AluOpType
ACT = mybir.ActivationFunctionType

P = 128
PACK = 4
K_PASS = P * PACK
WIDTH = 512
TILES = WIDTH // P
LIST_COLS = WIDTH // 16
QUADRANT = 32

SCALAR, VECTOR = "scalar", "vector"

WHOLE, FIRST, SECOND, QUARTER, REST = (0, 4), (0, 2), (2, 4), (0, 1), (1, 4)

OPERANDS = ("xg_0", "xg_1", "wp", "w1lo_0", "w1hi_0", "wx_0", "w1lo_1", "w1hi_1", "wx_1",
            "hid_0_0", "hid_0_1", "hid_1_0", "hid_1_1")
STAGING = (
    ("wx_0", "w1hi_1", "hid_1_1"),
    ("xg_1", "w1lo_1"),
    ("w1hi_0",),
    ("xg_0", "hid_0_0"),
    ("w1lo_0", "wp", "hid_1_0"),
    ("wx_1", "hid_0_1"),
)
RELU_BUFFER = {(0, 0): 2, (0, 1): 0, (1, 0): 1, (1, 1): 2}


def tile_list_contact_joint_gain_kernel(
    tc, tab_words, tab_scales, offs, xT, wgt, offs2, w1, wx, b1, w4_words, w4_scales, b2, wp, out
):
    nc = tc.nc
    with ExitStack() as ctx:
        lists = ctx.enter_context(tc.tile_pool(name="lists", bufs=1))
        keep = ctx.enter_context(tc.tile_pool(name="keep", bufs=1))
        psum = ctx.enter_context(tc.psum_pool(name="psum", bufs=1))

        tab_list = lists.tile([P, S // 16], U16, name="tab_list")
        x_lists = lists.tile([P, S // 16], U16, name="x_lists")

        x_plane = [keep.tile([P, T], F32, name=f"x_plane{j}", align_bytes=64) for j in range(PACK)]
        wgt_sb = keep.tile([P, S], F32, name="wgt_sb", align_bytes=64)
        tab_w = [keep.tile([P, T], I32, name=f"tab_w{a}", align_bytes=64) for a in range(2)]
        tab_s = keep.tile([P, T // 4], I32, name="tab_s", align_bytes=64)
        v_words = [keep.tile([P, S], U32, name=f"v_words{a}", align_bytes=64) for a in range(2)]
        v_scales = keep.tile([P, S], U8, name="v_scales", align_bytes=64)
        xg = [keep.tile([P, PACK, WIDTH], F32, name=f"xg{h}", align_bytes=64) for h in range(2)]
        w4_w = keep.tile([P, 2, 2 * N], U8, name="w4_w", align_bytes=64)
        w4_s = keep.tile([P, 2, N // 4], I32, name="w4_s", align_bytes=64)
        b1_sb = keep.tile([P, 2, PACK], F32, name="b1_sb", align_bytes=64)
        b2_sb = keep.tile([P, TILES], F32, name="b2_sb", align_bytes=64)
        result = keep.tile([P, 2, TILES, WIDTH], F32, name="result", align_bytes=64)

        codes = {n: keep.tile([P, WIDTH], U32, name=f"codes_{n}", align_bytes=64) for n in OPERANDS}
        scales = {n: keep.tile([P, WIDTH], U8, name=f"scales_{n}", align_bytes=64) for n in OPERANDS}
        raw = {n: keep.tile([P, PACK, WIDTH], F32, name=f"raw_{n}", align_bytes=64) for n in OPERANDS if n[0] == "w"}
        raw["xg_0"], raw["xg_1"] = xg
        staged = {}
        for slot, users in enumerate(STAGING):
            buffer = keep.tile([P, PACK * WIDTH], BF16, name=f"staging{slot}", align_bytes=64)
            for n in users:
                staged[n] = buffer
        relu_buffers = [keep.tile([P, PACK, WIDTH], BF16, name=f"relu{slot}", align_bytes=64) for slot in range(3)]
        banks = {(h, t): psum.tile([P, WIDTH], F32, name=f"bank{h}{t}") for h in range(2) for t in range(TILES)}

        def span(i):
            return slice(WIDTH * i, WIDTH * (i + 1))

        def load_x(j):
            nc.sync.dma_start(out=x_plane[j][:], in_=xT.rearrange("(p j) t -> p j t", j=PACK)[:, j, :])

        def load_wgt(h):
            nc.sync.dma_start(out=wgt_sb[:, span(h)], in_=wgt[:, span(h)])

        def load_table_words(a):
            nc.sync.dma_start(out=tab_w[a][:], in_=tab_words[a].rearrange("p t j -> p (t j)").bitcast(I32))

        def load_table_scales(q):
            rows = slice(QUADRANT * q, QUADRANT * q + 8)
            nc.sync.dma_start(out=tab_s[rows, :], in_=tab_scales[:, 4 * q : 4 * q + 4, :].bitcast(I32))

        def load_w4_words():
            nc.sync.dma_start(out=w4_w[:].bitcast(I32), in_=w4_words.rearrange("b p c -> p b c").bitcast(I32))

        def load_w4_scales(q):
            nc.sync.dma_start(
                out=w4_s[QUADRANT * q : QUADRANT * q + 4, :, :],
                in_=w4_scales[:, 4 * q : 4 * q + 4, :].bitcast(I32).rearrange("b r c -> r b c"),
            )

        def load_b1():
            nc.sync.dma_start(out=b1_sb[:], in_=b1.rearrange("(b p t) -> p b t", p=P, t=PACK))

        def load_b2():
            with nc.allow_non_contiguous_dma(reason="one bias value for each partition and output tile"):
                nc.sync.dma_start(out=b2_sb[:], in_=b2.rearrange("(t p) -> p t", p=P))

        weight_rows = {"wp": wp}
        for b in range(2):
            weight_rows[f"wx_{b}"] = wx[:, span(b)]
            weight_rows[f"w1lo_{b}"] = w1[:K_PASS, span(b)]
            weight_rows[f"w1hi_{b}"] = w1[K_PASS:, span(b)]

        def load_weight(name):
            nc.sync.dma_start(out=raw[name][:], in_=weight_rows[name].rearrange("(p j) c -> p j c", j=PACK))

        def gather_x(j, h):
            picked = x_plane[j][:].indirect(x_lists[:, LIST_COLS * h : LIST_COLS * (h + 1)])
            nc.vector.tensor_tensor(xg[h][:, j, :], picked, wgt_sb[:, span(h)], ALU.mult)

        def gather_words(a, h):
            picked = tab_w[a][:].bitcast(U32).indirect(tab_list[:, LIST_COLS * h : LIST_COLS * (h + 1)])
            nc.vector.tensor_copy(v_words[a][:, span(h)], picked)

        def gather_scales(h):
            picked = tab_s[:].bitcast(U8).indirect(tab_list[:, LIST_COLS * h : LIST_COLS * (h + 1)])
            nc.vector.tensor_copy(v_scales[:, span(h)], picked)

        def round_to_bf16(engine, dst, src):
            if engine == SCALAR:
                nc.scalar.activation(out=dst, in_=src, func=ACT.Copy)
            else:
                nc.vector.tensor_copy(out=dst, in_=src)

        def side_by_side(name, rows, part):
            groups = slice(part[0] * P // 4, part[1] * P // 4)
            dst = staged[name][:].rearrange("p (g i j) -> p g j i", i=4, j=PACK)[:, groups]
            return dst, rows[:].rearrange("p j (g i) -> p g j i", i=4)[:, groups]

        def round_columns(name, part, engine):
            round_to_bf16(engine, *side_by_side(name, raw[name], part))

        def round_tiles(name, part, engine):
            round_to_bf16(
                engine,
                staged[name][:].rearrange("p (t m j) -> p m j t", t=TILES, j=PACK)[:, :, :, part[0] : part[1]],
                raw[name][:].rearrange("p j (m t) -> p m j t", t=TILES)[:, :, :, part[0] : part[1]],
            )

        def quantize(name, part):
            c0, c1 = P * part[0], P * part[1]
            nc.vector.quantize_mx(
                out=codes[name][:, c0:c1].bitcast(FP8X4),
                scales=scales[name][:, c0:c1],
                in_=staged[name][:, PACK * c0 : PACK * c1],
            )

        def tile_of(name, t):
            c = slice(P * t, P * (t + 1))
            return codes[name][:, c].bitcast(FP8X4), scales[name][:, c]

        def all_columns(name):
            return codes[name][:].bitcast(FP8X4), scales[name][:]

        def table_pass(a, h):
            return v_words[a][:, span(h)].bitcast(FP8X4), v_scales[4 * a : P, span(h)]

        def multiply(bank, stationary, moving, start, stop):
            nc.tensor.matmul_mx(
                out=bank[:], lhsT=stationary[0], lhsT_scale=stationary[1], rhs=moving[0], rhs_scale=moving[1],
                start=start, stop=stop,
            )

        def hidden_pass(weight, b, h):
            moving = {"wx": all_columns(f"xg_{h}"), "w1lo": table_pass(0, h), "w1hi": table_pass(1, h)}[weight]
            for t in range(TILES):
                multiply(banks[h, t], tile_of(f"{weight}_{b}", t), moving, weight == "wx", weight == "w1hi")

        def relu(b, h, t, part, engine):
            c = slice(P * part[0], P * part[1])
            dst = relu_buffers[RELU_BUFFER[b, h]][:, t, c]
            bias = b1_sb[:, b, t : t + 1]
            if engine == SCALAR:
                nc.scalar.activation(out=dst, in_=banks[h, t][:, c], func=ACT.Relu, bias=bias)
            else:
                nc.vector.tensor_scalar(dst, banks[h, t][:, c], bias, 0.0, ALU.add, ALU.max)

        def interleave(b, h, part, engine):
            dst, src = side_by_side(f"hid_{b}_{h}", relu_buffers[RELU_BUFFER[b, h]], part)
            if engine == SCALAR:
                nc.scalar.copy(out=dst, in_=src)
            else:
                nc.vector.tensor_copy(out=dst, in_=src)

        def project(h, t):
            multiply(banks[h, t], tile_of("wp", t), all_columns(f"xg_{h}"), True, True)

        def keep_projection(h, t):
            nc.scalar.copy(out=result[:, h, t, :], in_=banks[h, t][:])

        def gain_pass(b, h):
            for t in range(TILES):
                w4_tile = (
                    w4_w[:, b, 2 * P * t : 2 * P * (t + 1)].bitcast(FP4X4),
                    w4_s[:, b, P // 4 * t : P // 4 * (t + 1)].bitcast(U8),
                )
                multiply(banks[h, t], w4_tile, all_columns(f"hid_{b}_{h}"), b == 0, b == 1)

        def finish(h, t):
            res = result[:, h, t, :]
            nc.vector.scalar_tensor_tensor(
                out=res, in0=banks[h, t][:], scalar=b2_sb[:, t : t + 1], in1=res, op0=ALU.add, op1=ALU.mult
            )
            nc.sync.dma_start(out=out[P * t : P * (t + 1), span(h)], in_=res)

        nc.vector.memset(tab_s[:], 0)
        nc.vector.memset(w4_s[:], 0)


        load_wgt(1)
        nc.sync.dma_start(x_lists[:], offs2)
        load_x(0)
        load_table_scales(0)
        load_x(1)
        load_wgt(0)
        load_b1()
        nc.sync.dma_start(tab_list[:], offs)
        load_x(2)
        load_x(3)
        load_table_words(0)
        load_weight("wx_0")
        load_table_scales(1)
        load_table_scales(2)
        load_weight("w1lo_0")
        load_table_scales(3)
        load_table_words(1)
        load_weight("w1hi_0")
        load_weight("wx_1")
        load_weight("w1lo_1")
        load_weight("w1hi_1")
        load_weight("wp")
        load_w4_scales(0)
        load_w4_scales(1)
        load_w4_scales(2)
        load_w4_words()
        load_w4_scales(3)
        load_b2()

        gather_x(0, 1)
        gather_x(1, 1)
        gather_x(1, 0)
        gather_x(0, 0)
        gather_x(2, 1)
        gather_x(2, 0)
        gather_x(3, 1)
        gather_x(3, 0)
        round_columns("xg_1", FIRST, SCALAR)
        round_columns("xg_0", QUARTER, VECTOR)
        round_columns("xg_0", REST, SCALAR)
        quantize("xg_1", FIRST)
        gather_words(0, 0)
        gather_words(0, 1)
        round_columns("xg_1", SECOND, SCALAR)
        quantize("xg_0", WHOLE)
        quantize("xg_1", SECOND)

        round_tiles("wx_0", FIRST, VECTOR)
        round_tiles("wx_0", SECOND, VECTOR)
        round_tiles("w1lo_0", WHOLE, SCALAR)
        quantize("wx_0", FIRST)
        quantize("wx_0", SECOND)
        hidden_pass("wx", 0, 0)
        gather_scales(0)
        gather_scales(1)
        hidden_pass("wx", 0, 1)
        quantize("w1lo_0", WHOLE)
        gather_words(1, 1)
        hidden_pass("w1lo", 0, 1)
        round_tiles("w1hi_0", SECOND, SCALAR)
        gather_words(1, 0)
        hidden_pass("w1lo", 0, 0)
        round_tiles("w1hi_0", FIRST, SCALAR)
        quantize("w1hi_0", FIRST)
        quantize("w1hi_0", SECOND)

        round_tiles("wx_1", FIRST, VECTOR)
        round_tiles("wx_1", SECOND, SCALAR)
        hidden_pass("w1hi", 0, 0)
        relu(0, 0, 2, WHOLE, SCALAR)
        relu(0, 0, 3, WHOLE, VECTOR)
        hidden_pass("w1hi", 0, 1)
        quantize("wx_1", FIRST)
        relu(0, 0, 1, WHOLE, SCALAR)
        quantize("wx_1", SECOND)
        round_tiles("w1lo_1", FIRST, VECTOR)
        relu(0, 0, 0, WHOLE, SCALAR)
        relu(0, 1, 0, WHOLE, SCALAR)
        round_tiles("w1lo_1", SECOND, VECTOR)
        hidden_pass("wx", 1, 0)
        relu(0, 1, 1, WHOLE, SCALAR)
        interleave(0, 0, WHOLE, VECTOR)
        relu(0, 1, 2, WHOLE, SCALAR)
        relu(0, 1, 3, WHOLE, SCALAR)
        hidden_pass("wx", 1, 1)
        round_tiles("w1hi_1", FIRST, VECTOR)
        interleave(0, 1, WHOLE, SCALAR)
        quantize("w1lo_1", FIRST)
        quantize("w1hi_1", FIRST)
        quantize("hid_0_0", WHOLE)
        round_tiles("w1hi_1", SECOND, VECTOR)
        quantize("w1lo_1", SECOND)
        hidden_pass("w1lo", 1, 0)
        hidden_pass("w1lo", 1, 1)

        round_columns("wp", REST, SCALAR)
        round_columns("wp", QUARTER, VECTOR)
        quantize("w1hi_1", SECOND)
        hidden_pass("w1hi", 1, 0)
        hidden_pass("w1hi", 1, 1)
        relu(1, 0, 0, WHOLE, VECTOR)
        relu(1, 0, 1, WHOLE, VECTOR)
        relu(1, 1, 0, FIRST, SCALAR)
        quantize("hid_0_1", WHOLE)
        relu(1, 1, 1, SECOND, SCALAR)
        relu(1, 1, 1, FIRST, SCALAR)
        quantize("wp", WHOLE)
        relu(1, 1, 0, SECOND, SCALAR)
        relu(1, 0, 3, WHOLE, SCALAR)
        relu(1, 0, 2, WHOLE, VECTOR)

        project(0, 1)
        project(0, 0)
        relu(1, 1, 2, FIRST, SCALAR)
        relu(1, 1, 3, SECOND, VECTOR)
        project(0, 3)
        interleave(1, 0, WHOLE, VECTOR)
        relu(1, 1, 2, SECOND, SCALAR)
        project(0, 2)
        keep_projection(0, 1)
        project(1, 1)
        project(1, 0)
        interleave(1, 1, SECOND, SCALAR)
        project(1, 2)
        relu(1, 1, 3, FIRST, VECTOR)
        quantize("hid_1_0", WHOLE)
        project(1, 3)
        keep_projection(0, 3)
        interleave(1, 1, FIRST, VECTOR)
        keep_projection(0, 2)
        quantize("hid_1_1", SECOND)
        keep_projection(0, 0)
        quantize("hid_1_1", FIRST)
        keep_projection(1, 1)

        gain_pass(0, 0)
        keep_projection(1, 0)
        gain_pass(1, 0)
        finish(0, 1)
        finish(0, 3)
        finish(0, 2)
        keep_projection(1, 3)
        finish(0, 0)
        keep_projection(1, 2)
        gain_pass(0, 1)
        gain_pass(1, 1)
        finish(1, 1)
        finish(1, 0)
        finish(1, 3)
        finish(1, 2)
